import numpy as np
import ml_dtypes


def mxq(x, axis, fmt="e4m3"):
    dtype, down = {"e4m3": (ml_dtypes.float8_e4m3fn, 7), "e5m2": (ml_dtypes.float8_e5m2, 14)}[fmt]
    v = np.moveaxis(np.asarray(x, np.float32).astype(ml_dtypes.bfloat16).astype(np.float64), axis, -1)
    blocks = v.reshape(v.shape[:-1] + (-1, 32))
    amax = np.abs(blocks).max(-1, keepdims=True)
    byte = np.maximum(np.where(amax > 0, np.frexp(amax)[1] - 1 + 127, 0) - down, 1)
    scale = np.exp2(byte - 127.0)
    codes = (blocks / scale).astype(np.float32).astype(dtype).astype(np.float64)
    return np.moveaxis((codes * scale).reshape(v.shape), -1, axis)


WIDE = False


def mx_kscale(k):
    if not WIDE:
        return np.ones(k)
    levels = np.array([30, -30])
    if k % 512:
        return np.exp2(np.random.permutation(np.resize(levels, k // 32))).repeat(32)
    a = np.empty((k // 512, 16))
    for p in range(k // 512):
        a[p, :8] = np.random.permutation(np.resize(levels, 8))
        for g in range(8):
            far = levels[np.abs(levels - a[p, g]) >= 10]
            a[p, g + 8] = far[np.random.randint(len(far))]
    return np.exp2(a.ravel()).repeat(32)


def f64(x):
    return np.asarray(x).astype(np.float64)


def striped(idx):
    return np.tile(np.asarray(idx).reshape(-1, 16).T, (8, 1)).astype(np.uint16)


def unstriped(offs):
    return offs[:16].T.reshape(-1).astype(np.int64)


E2M1 = np.array([0.0, 0.5, 1.0, 1.5, 2.0, 3.0, 4.0, 6.0, -0.0, -0.5, -1.0, -1.5, -2.0, -3.0, -4.0, -6.0])


def pack_weight(w, fmt):
    k, n = w.shape
    w = f64(np.asarray(w, np.float32).astype(ml_dtypes.bfloat16)).reshape(k // 32, 32, n)
    amax = np.abs(w).max(1)
    if fmt in ("e4m3", "e5m2"):
        byte = np.frexp(amax)[1] - 1 + 127 - (7 if fmt == "e4m3" else 14)
    else:
        mant, ex = np.frexp(amax / 6.0)
        byte = np.where(mant > 0.5, ex, ex - 1) + 127
    byte = np.clip(np.where(amax > 0, byte, 1), 1, 254)
    scaled = (w * np.exp2(127.0 - byte)[:, None, :]).reshape(k, n).astype(np.float32)
    by_word = np.ascontiguousarray(scaled.reshape(k // 512, 128, 4, n).transpose(0, 1, 3, 2))
    if fmt in ("e4m3", "e5m2"):
        words = by_word.astype(ml_dtypes.float8_e4m3fn if fmt == "e4m3" else ml_dtypes.float8_e5m2).view(np.uint8)
    else:
        c = by_word.astype(ml_dtypes.float4_e2m1fn).view(np.uint8) & 0xF
        words = (c[..., 0::2] | (c[..., 1::2] << 4)).reshape(k // 512, 128, 2 * n)
    return np.ascontiguousarray(words), np.ascontiguousarray(byte.astype(np.uint8).reshape(k // 512, 16, n))


def unpack_weight(words, scales, fmt):
    g, _, n = scales.shape
    words = np.ascontiguousarray(words).reshape(g, 128, n, -1)
    if fmt in ("e4m3", "e5m2"):
        vals = words.view(ml_dtypes.float8_e4m3fn if fmt == "e4m3" else ml_dtypes.float8_e5m2).astype(np.float64)
    else:
        nib = np.empty((g, 128, n, 4), np.uint8)
        nib[..., 0::2] = words & 0xF
        nib[..., 1::2] = words >> 4
        vals = E2M1[nib]
    vals = vals * np.repeat(np.exp2(scales.astype(np.float64) - 127.0), 8, axis=1)[..., None]
    return vals.transpose(0, 1, 3, 2).reshape(g * 512, n)


def sigmoid(v):
    return 1.0 / (1.0 + np.exp(-v))


K, F, T, Z, J, R, O, N, E = 512, 512, 1024, 1024, 256, 512, 128, 256, 512


def setup_inputs():
    n = np.random.standard_normal
    idx = np.random.permutation(T)[:J]
    idx2 = np.random.permutation(Z)[:J]
    idx3 = np.random.permutation(J)[:O]
    idx4 = np.random.permutation(J)[:O]
    idx5 = np.random.permutation(E)[:O]
    fk = mx_kscale(K)
    ff = mx_kscale(F)
    fr = mx_kscale(R)
    xtp = pack_weight(n((K, T)) / fk[:, None], "e2m1")
    wp = pack_weight(n((K, R)) * 1 / np.sqrt(K) * fk[:, None], "e5m2")
    xop = pack_weight(n((F, Z)) / ff[:, None], "e5m2")
    w2p = pack_weight(n((F, R)) * 1 / np.sqrt(F) * ff[:, None] * fr, "e4m3")
    wbp = pack_weight(n((R, N)) * 1 / np.sqrt(R) / fr[:, None], "e4m3")
    return {
        "xt_words": xtp[0],
        "xt_scales": xtp[1],
        "w_words": wp[0],
        "w_scales": wp[1],
        "xo_words": xop[0],
        "xo_scales": xop[1],
        "w2_words": w2p[0],
        "w2_scales": w2p[1],
        "sg": (np.random.uniform(0.6, 1.6, (R, 1))).astype(np.float32),
        "wb_words": wbp[0],
        "wb_scales": wbp[1],
        "tz": (n((N, E))).astype(np.float32),
        "so": (np.random.uniform(0.6, 1.6, (N, 1))).astype(np.float32),
        "bo": (np.random.uniform(-1.0, 1.0, (N, 1))).astype(np.float32),
        "offs": striped(idx),
        "offs2": striped(idx2),
        "offs3": striped(idx3),
        "offs4": striped(idx4),
        "offs5": striped(idx5),
    }


def reference(xt_words, xt_scales, w_words, w_scales, xo_words, xo_scales, w2_words, w2_scales, sg, wb_words, wb_scales, tz, so, bo, offs, offs2, offs3, offs4, offs5):
    idx = unstriped(offs)
    idx2 = unstriped(offs2)
    idx3 = unstriped(offs3)
    idx4 = unstriped(offs4)
    idx5 = unstriped(offs5)
    xtu = unpack_weight(xt_words, xt_scales, "e2m1")
    wu = unpack_weight(w_words, w_scales, "e5m2")
    xou = unpack_weight(xo_words, xo_scales, "e5m2")
    w2u = unpack_weight(w2_words, w2_scales, "e4m3")
    wbu = unpack_weight(wb_words, wb_scales, "e4m3")
    xtidxg = xtu[:, idx]
    a = wu.T @ xtidxg
    xoidx2g = xou[:, idx2]
    b = w2u.T @ xoidx2g
    hid = np.maximum(b[:, idx3], b[:, idx4]) * sigmoid(a[:, idx4] * f64(sg))
    hidq = mxq(hid, 0, "e5m2")
    p = wbu.T @ hidq
    y = p * sigmoid(f64(tz)[:, idx5] * f64(so) + f64(bo))
    return y

@@ -1,0 +1,170 @@
+from contextlib import ExitStack
+
+import concourse.mybir as mybir
+
+K, F, T, Z, J, R, O, N, E = 512, 512, 1024, 1024, 256, 512, 128, 256, 512
+FLOPS = 2 * (K * R * J + F * R * J + R * N * O)
+
+F32 = mybir.dt.float32
+BF16 = mybir.dt.bfloat16
+I32 = mybir.dt.int32
+U32 = mybir.dt.uint32
+U16 = mybir.dt.uint16
+U8 = mybir.dt.uint8
+E4M3 = mybir.dt.float8_e4m3fn_x4
+E5M2 = mybir.dt.float8_e5m2_x4
+E2M1 = mybir.dt.float4_e2m1fn_x4
+ACT = mybir.ActivationFunctionType
+ALU = mybir.AluOpType
+
+P = 128
+PACK = 4
+ALIGN = 64
+
+
+def tile_list_twotab_agree_one_finalgate_kernel(
+    tc, xt_words, xt_scales, w_words, w_scales, xo_words, xo_scales, w2_words, w2_scales,
+    sg, wb_words, wb_scales, tz, so, bo, offs, offs2, offs3, offs4, offs5, out,
+):
+    nc = tc.nc
+    with ExitStack() as ctx:
+        pool = ctx.enter_context(tc.tile_pool(name="keep", bufs=1))
+        psum = ctx.enter_context(tc.psum_pool(name="psum", bufs=8))
+
+        def sb(name, shape, dtype):
+            return pool.tile(shape, dtype, name=name, align_bytes=ALIGN)
+
+        def load_list(name, src):
+            tile = pool.tile(list(src.shape), U16, name=name)
+            nc.sync.dma_start(tile[:], src)
+            return tile
+
+        def load_words(eng, name, src, width):
+            tile = sb(name, [P, width], U32)
+            eng.dma_start(out=tile[:].bitcast(I32), in_=src[0].rearrange("p n t -> p (n t)").bitcast(I32))
+            return tile
+
+        def scale_tile(eng, name, width):
+            tile = sb(name, [P, width], U8)
+            eng.memset(tile[:].bitcast(I32), 0)
+            return tile
+
+        def load_scales(engs, tile, src):
+            for q in range(4):
+                engs[q].dma_start(
+                    out=tile[32 * q : 32 * q + 4, :].bitcast(I32),
+                    in_=src[0, 4 * q : 4 * q + 4, :].bitcast(I32),
+                )
+
+        sy, sc, gp = nc.sync, nc.scalar, nc.gpsimd
+        xt_s = scale_tile(gp, "xt_s", T)
+        w2_s = scale_tile(gp, "w2_s", R)
+        w_s = scale_tile(nc.vector, "w_s", R)
+        xo_s = scale_tile(nc.vector, "xo_s", Z)
+        wb_s = scale_tile(nc.vector, "wb_s", N)
+        l1 = load_list("l1", offs)
+        load_scales([sy, sc, sy, sc], xt_s, xt_scales)
+        xt_w = sb("xt_w", [P, T], U16)
+        sy.dma_start(out=xt_w[:].bitcast(I32), in_=xt_words[0].bitcast(I32))
+        w_w = load_words(sc, "w_w", w_words, R)
+        load_scales([sy, sy, sy, sy], w_s, w_scales)
+        load_scales([gp, gp, gp, gp], w2_s, w2_scales)
+        l2 = load_list("l2", offs2)
+        xo_w = load_words(sy, "xo_w", xo_words, Z)
+        w2_w = load_words(sy, "w2_w", w2_words, R)
+        load_scales([sy, sy, sy, sy], xo_s, xo_scales)
+        l4 = load_list("l4", offs4)
+        sg_t = sb("sg_t", [P, PACK], F32)
+        sy.dma_start(out=sg_t[:], in_=sg.rearrange("(p t) o -> p (t o)", t=PACK))
+        l3 = load_list("l3", offs3)
+        l5 = load_list("l5", offs5)
+        tz_t = [sb("tz%d" % h, [P, E], F32) for h in range(2)]
+        so_t = sb("so_t", [P, 2], F32)
+        bo_t = sb("bo_t", [P, 2], F32)
+        for h in range(2):
+            sy.dma_start(out=tz_t[h][:], in_=tz[h * P : (h + 1) * P, :])
+        with nc.allow_non_contiguous_dma(reason="one value a partition"):
+            sy.dma_start(out=so_t[:], in_=so.rearrange("(h p) o -> p (h o)", h=2))
+            sy.dma_start(out=bo_t[:], in_=bo.rearrange("(h p) o -> p (h o)", h=2))
+        wb_w = load_words(sy, "wb_w", wb_words, N)
+        load_scales([sy, sy, sy, sy], wb_s, wb_scales)
+
+        def deal(eng, name, src, dtype):
+            tile = sb(name, [P, PACK, P], dtype)
+            dst = tile[:].rearrange("p t m -> p m t")
+            words = src[:].rearrange("p (m t) -> p m t", t=PACK)
+            if eng is sc:
+                eng.copy(out=dst, in_=words)
+            else:
+                eng.tensor_copy(out=dst, in_=words)
+            return tile
+
+        def gather(name, src, lst, dtype, n):
+            tile = sb(name, [P, n], dtype)
+            nc.vector.tensor_copy(out=tile[:], in_=src[:].indirect(lst[:]))
+            return tile
+
+        w_wd = deal(sc, "w_wd", w_w, U32)
+        xt_g = gather("xt_g", xt_w, l1, U16, J)
+        xt_sg = gather("xt_sg", xt_s, l1, U8, J)
+        w_sd = deal(nc.vector, "w_sd", w_s, U8)
+        a_sb = [sb("a%d" % t, [P, J], F32) for t in range(PACK)]
+        sig = sb("sig", [P, PACK, O], F32)
+        for t in range(PACK):
+            acc = psum.tile([P, J], F32, name="acc")
+            nc.tensor.matmul_mx(out=acc[:], lhsT=w_wd[:, t, :].bitcast(E5M2), lhsT_scale=w_sd[:, t, :],
+                                rhs=xt_g[:].bitcast(E2M1), rhs_scale=xt_sg[:], start=True, stop=True)
+            nc.scalar.copy(out=a_sb[t][:], in_=acc[:])
+        for t in range(PACK):
+            nc.scalar.activation(out=sig[:, t, :], in_=a_sb[t][:].indirect(l4[:]), func=ACT.Sigmoid,
+                                 scale=sg_t[:, t : t + 1])
+
+        w2_wd = deal(sc, "w2_wd", w2_w, U32)
+        xo_g = gather("xo_g", xo_w, l2, U32, J)
+        w2_sd = deal(nc.vector, "w2_sd", w2_s, U8)
+        xo_sg = gather("xo_sg", xo_s, l2, U8, J)
+        b_sb = [sb("b%d" % t, [P, J], F32) for t in range(PACK)]
+        u = sb("u", [P, PACK, O], F32)
+        v = sb("v", [P, PACK, O], F32)
+        for t in range(PACK):
+            acc = psum.tile([P, J], F32, name="acc")
+            nc.tensor.matmul_mx(out=acc[:], lhsT=w2_wd[:, t, :].bitcast(E4M3), lhsT_scale=w2_sd[:, t, :],
+                                rhs=xo_g[:].bitcast(E5M2), rhs_scale=xo_sg[:], start=True, stop=True)
+            nc.vector.tensor_copy(out=b_sb[t][:], in_=acc[:])
+        for t in range(PACK):
+            nc.scalar.activation(out=v[:, t, :], in_=b_sb[t][:].indirect(l4[:]), func=ACT.Copy)
+            if t == 2:
+                nc.scalar.activation(out=u[:, t, :], in_=b_sb[t][:].indirect(l3[:]), func=ACT.Copy)
+            else:
+                nc.vector.tensor_copy(out=u[:, t, :], in_=b_sb[t][:].indirect(l3[:]))
+
+        gate = sb("gate", [P, 2, O], F32)
+        for h in range(2):
+            nc.scalar.activation(out=gate[:, h, :], in_=tz_t[h][:].indirect(l5[:]), func=ACT.Sigmoid,
+                                 bias=bo_t[:, h : h + 1], scale=so_t[:, h : h + 1])
+
+        big = sb("big", [P, PACK, O], F32)
+        for t in range(0, PACK, 2):
+            nc.vector.tensor_tensor(out=big[:, t : t + 2, :], in0=u[:, t : t + 2, :], in1=v[:, t : t + 2, :], op=ALU.max)
+        hid = sb("hid", [P, O, PACK], BF16)
+        hid_w = sb("hid_w", [P, O], U32)
+        hid_s = sb("hid_s", [P, O], U8)
+        H = O // 2
+        for c in range(2):
+            cols = slice(c * H, (c + 1) * H)
+            nc.vector.tensor_tensor(out=hid[:, cols, :], in0=big[:, :, cols].rearrange("p t o -> p o t"),
+                                    in1=sig[:, :, cols].rearrange("p t o -> p o t"), op=ALU.mult)
+        for c in range(2):
+            cols = slice(c * H, (c + 1) * H)
+            nc.vector.quantize_mx(out=hid_w[:, cols].bitcast(E5M2), scales=hid_s[:, cols],
+                                  in_=hid[:, cols, :].rearrange("p o t -> p (o t)"))
+
+        res = sb("res", [P, 2, O], F32)
+        acc = psum.tile([P, J], F32, name="acc")
+        for h in range(2):
+            nc.tensor.matmul_mx(out=acc[:, h * O : (h + 1) * O], lhsT=wb_w[:, h * P : (h + 1) * P].bitcast(E4M3),
+                                lhsT_scale=wb_s[:, h * P : (h + 1) * P],
+                                rhs=hid_w[:].bitcast(E5M2), rhs_scale=hid_s[:], start=True, stop=True)
+        nc.vector.tensor_tensor(out=res[:].rearrange("p h o -> p (h o)"), in0=acc[:],
+                                in1=gate[:].rearrange("p h o -> p (h o)"), op=ALU.mult)
+        nc.sync.dma_start(out=out.rearrange("(h p) o -> p h o", h=2), in_=res[:])

@@ -31,16 +31,16 @@ def tile_list_twotab_agree_one_finalgate_kernel(
         pool = ctx.enter_context(tc.tile_pool(name="keep", bufs=1))
         psum = ctx.enter_context(tc.psum_pool(name="psum", bufs=8))
 
-        def sb(name, shape, dtype):
-            return pool.tile(shape, dtype, name=name, align_bytes=ALIGN)
+        def sb(name, shape, dtype, tag=""):
+            return pool.tile(shape, dtype, name=name, align_bytes=ALIGN, tag=tag)
 
         def load_list(name, src):
             tile = pool.tile(list(src.shape), U16, name=name)
             nc.sync.dma_start(tile[:], src)
             return tile
 
-        def load_words(eng, name, src, width):
-            tile = sb(name, [P, width], U32)
+        def load_words(eng, name, src, width, tag=""):
+            tile = sb(name, [P, width], U32, tag=tag)
             eng.dma_start(out=tile[:].bitcast(I32), in_=src[0].rearrange("p n t -> p (n t)").bitcast(I32))
             return tile
 
@@ -56,41 +56,35 @@ def tile_list_twotab_agree_one_finalgate_kernel(
                     in_=src[0, 4 * q : 4 * q + 4, :].bitcast(I32),
                 )
 
-        sy, sc, gp = nc.sync, nc.scalar, nc.gpsimd
-        xt_s = scale_tile(gp, "xt_s", T)
+        sy, sc, gp, ve = nc.sync, nc.scalar, nc.gpsimd, nc.vector
+        xo_s = scale_tile(ve, "xo_s", Z)
         w2_s = scale_tile(gp, "w2_s", R)
-        w_s = scale_tile(nc.vector, "w_s", R)
-        xo_s = scale_tile(nc.vector, "xo_s", Z)
-        wb_s = scale_tile(nc.vector, "wb_s", N)
-        l1 = load_list("l1", offs)
-        load_scales([sy, sc, sy, sc], xt_s, xt_scales)
-        xt_w = sb("xt_w", [P, T], U16)
-        sy.dma_start(out=xt_w[:].bitcast(I32), in_=xt_words[0].bitcast(I32))
-        w_w = load_words(sc, "w_w", w_words, R)
-        load_scales([sy, sy, sy, sy], w_s, w_scales)
-        load_scales([gp, gp, gp, gp], w2_s, w2_scales)
+        xt_s = scale_tile(ve, "xt_s", T)
+        w_s = scale_tile(gp, "w_s", R)
+        wb_s = scale_tile(ve, "wb_s", N)
+        warm = sb("warm", [P, 2], F32)
+        nc.gpsimd.memset(warm[:, 0:1], 0.0)
+        nc.scalar.activation(out=warm[:, 1:2], in_=warm[:, 0:1], func=ACT.Sigmoid)
+
         l2 = load_list("l2", offs2)
         xo_w = load_words(sy, "xo_w", xo_words, Z)
-        w2_w = load_words(sy, "w2_w", w2_words, R)
+        w2_w = load_words(sc, "w2_w", w2_words, R)
         load_scales([sy, sy, sy, sy], xo_s, xo_scales)
+        load_scales([sy, sy, sy, sy], w2_s, w2_scales)
+        l1 = load_list("l1", offs)
+        xt_w = sb("xt_w", [P, T], U16)
+        sy.dma_start(out=xt_w[:].bitcast(I32), in_=xt_words[0].bitcast(I32))
+        w_w = load_words(sy, "w_w", w_words, R)
         l4 = load_list("l4", offs4)
-        sg_t = sb("sg_t", [P, PACK], F32)
-        sy.dma_start(out=sg_t[:], in_=sg.rearrange("(p t) o -> p (t o)", t=PACK))
         l3 = load_list("l3", offs3)
-        l5 = load_list("l5", offs5)
-        tz_t = [sb("tz%d" % h, [P, E], F32) for h in range(2)]
-        so_t = sb("so_t", [P, 2], F32)
-        bo_t = sb("bo_t", [P, 2], F32)
-        for h in range(2):
-            sy.dma_start(out=tz_t[h][:], in_=tz[h * P : (h + 1) * P, :])
-        with nc.allow_non_contiguous_dma(reason="one value a partition"):
-            sy.dma_start(out=so_t[:], in_=so.rearrange("(h p) o -> p (h o)", h=2))
-            sy.dma_start(out=bo_t[:], in_=bo.rearrange("(h p) o -> p (h o)", h=2))
-        wb_w = load_words(sy, "wb_w", wb_words, N)
-        load_scales([sy, sy, sy, sy], wb_s, wb_scales)
+        load_scales([sy, sy, sy, sy], xt_s, xt_scales)
+        load_scales([sy, sy, sy, sy], w_s, w_scales)
+        sg_t = sb("sg_t", [P, PACK], F32)
+        gp.dma_start(out=sg_t[:], in_=sg.rearrange("(p t) o -> p (t o)", t=PACK))
+        load_scales([sy,sy,sy,sy], wb_s, wb_scales)
 
-        def deal(eng, name, src, dtype):
-            tile = sb(name, [P, PACK, P], dtype)
+        def deal(eng, name, src, dtype, tag=""):
+            tile = pool.tile([P, PACK, P], dtype, name=name, align_bytes=ALIGN, tag=tag)
             dst = tile[:].rearrange("p t m -> p m t")
             words = src[:].rearrange("p (m t) -> p m t", t=PACK)
             if eng is sc:
@@ -101,51 +95,61 @@ def tile_list_twotab_agree_one_finalgate_kernel(
 
         def gather(name, src, lst, dtype, n):
             tile = sb(name, [P, n], dtype)
-            nc.vector.tensor_copy(out=tile[:], in_=src[:].indirect(lst[:]))
+            ve.tensor_copy(out=tile[:], in_=src[:].indirect(lst[:]))
             return tile
-
-        w_wd = deal(sc, "w_wd", w_w, U32)
-        xt_g = gather("xt_g", xt_w, l1, U16, J)
-        xt_sg = gather("xt_sg", xt_s, l1, U8, J)
-        w_sd = deal(nc.vector, "w_sd", w_s, U8)
-        a_sb = [sb("a%d" % t, [P, J], F32) for t in range(PACK)]
-        sig = sb("sig", [P, PACK, O], F32)
-        for t in range(PACK):
-            acc = psum.tile([P, J], F32, name="acc")
-            nc.tensor.matmul_mx(out=acc[:], lhsT=w_wd[:, t, :].bitcast(E5M2), lhsT_scale=w_sd[:, t, :],
-                                rhs=xt_g[:].bitcast(E2M1), rhs_scale=xt_sg[:], start=True, stop=True)
-            nc.scalar.copy(out=a_sb[t][:], in_=acc[:])
-        for t in range(PACK):
-            nc.scalar.activation(out=sig[:, t, :], in_=a_sb[t][:].indirect(l4[:]), func=ACT.Sigmoid,
-                                 scale=sg_t[:, t : t + 1])
 
         w2_wd = deal(sc, "w2_wd", w2_w, U32)
         xo_g = gather("xo_g", xo_w, l2, U32, J)
-        w2_sd = deal(nc.vector, "w2_sd", w2_s, U8)
         xo_sg = gather("xo_sg", xo_s, l2, U8, J)
+        w2_sd = deal(ve, "w2_sd", w2_s, U8)
+        w_wd = deal(sc, "w_wd", w_w, U32)
+        xt_g = gather("xt_g", xt_w, l1, U16, J)
+        xt_sg = gather("xt_sg", xt_s, l1, U8, J)
+        w_sd = deal(ve, "w_sd", w_s, U8)
+
+        wb_w = load_words(sy, "wb_w", wb_words, N, tag="w2_s")
+        l5 = load_list("l5", offs5)
+        tz_t = [sb("tz%d" % h, [P, E], F32, tag=("w2_w", "w_w")[h]) for h in range(2)]
+        so_t = sb("so_t", [P, 2], F32)
+        bo_t = sb("bo_t", [P, 2], F32)
+        for h in range(2):
+            sy.dma_start(out=tz_t[h][:], in_=tz[h * P : (h + 1) * P, :])
+        with nc.allow_non_contiguous_dma(reason="one value a partition"):
+            gp.dma_start(out=so_t[:], in_=so.rearrange("(h p) o -> p (h o)", h=2))
+            gp.dma_start(out=bo_t[:], in_=bo.rearrange("(h p) o -> p (h o)", h=2))
+
         b_sb = [sb("b%d" % t, [P, J], F32) for t in range(PACK)]
-        u = sb("u", [P, PACK, O], F32)
+        a_sb = [sb("a%d" % t, [P, J], F32) for t in range(PACK)]
+        u = sb("u", [P, PACK, O], F32, tag="w_s")
         v = sb("v", [P, PACK, O], F32)
+        sig = sb("sig", [P, PACK, O], F32)
+        big = sb("big", [P, PACK, O], F32)
         for t in range(PACK):
             acc = psum.tile([P, J], F32, name="acc")
             nc.tensor.matmul_mx(out=acc[:], lhsT=w2_wd[:, t, :].bitcast(E4M3), lhsT_scale=w2_sd[:, t, :],
                                 rhs=xo_g[:].bitcast(E5M2), rhs_scale=xo_sg[:], start=True, stop=True)
-            nc.vector.tensor_copy(out=b_sb[t][:], in_=acc[:])
+            sc.copy(out=b_sb[t][:], in_=acc[:])
         for t in range(PACK):
-            nc.scalar.activation(out=v[:, t, :], in_=b_sb[t][:].indirect(l4[:]), func=ACT.Copy)
-            if t == 2:
-                nc.scalar.activation(out=u[:, t, :], in_=b_sb[t][:].indirect(l3[:]), func=ACT.Copy)
+            acc = psum.tile([P, J], F32, name="acc")
+            nc.tensor.matmul_mx(out=acc[:], lhsT=w_wd[:, t, :].bitcast(E5M2), lhsT_scale=w_sd[:, t, :],
+                                rhs=xt_g[:].bitcast(E2M1), rhs_scale=xt_sg[:], start=True, stop=True)
+            ve.tensor_copy(out=a_sb[t][:], in_=acc[:])
+        for t in range(PACK):
+            sc.activation(out=v[:, t, :], in_=b_sb[t][:].indirect(l4[:]), func=ACT.Copy)
+            if t == 3:
+                sc.activation(out=u[:, t, :], in_=b_sb[t][:].indirect(l3[:]), func=ACT.Copy)
             else:
-                nc.vector.tensor_copy(out=u[:, t, :], in_=b_sb[t][:].indirect(l3[:]))
-
-        gate = sb("gate", [P, 2, O], F32)
-        for h in range(2):
-            nc.scalar.activation(out=gate[:, h, :], in_=tz_t[h][:].indirect(l5[:]), func=ACT.Sigmoid,
-                                 bias=bo_t[:, h : h + 1], scale=so_t[:, h : h + 1])
-
-        big = sb("big", [P, PACK, O], F32)
+                ve.tensor_copy(out=u[:, t, :], in_=b_sb[t][:].indirect(l3[:]))
+        for t in range(PACK):
+            sc.activation(out=sig[:, t, :], in_=a_sb[t][:].indirect(l4[:]), func=ACT.Sigmoid,
+                          scale=sg_t[:, t : t + 1])
         for t in range(0, PACK, 2):
-            nc.vector.tensor_tensor(out=big[:, t : t + 2, :], in0=u[:, t : t + 2, :], in1=v[:, t : t + 2, :], op=ALU.max)
+            ve.tensor_tensor(out=big[:, t : t + 2, :], in0=u[:, t : t + 2, :], in1=v[:, t : t + 2, :], op=ALU.max)
+
+        gate = sb("gate", [P, 2, O], F32, tag="sg_t")
+        for h in range(2):
+            sc.activation(out=gate[:, h, :], in_=tz_t[h][:].indirect(l5[:]), func=ACT.Sigmoid,
+                          bias=bo_t[:, h : h + 1], scale=so_t[:, h : h + 1])
         hid = sb("hid", [P, O, PACK], BF16)
         hid_w = sb("hid_w", [P, O], U32)
         hid_s = sb("hid_s", [P, O], U8)

@@ -19,7 +19,12 @@ ALU = mybir.AluOpType
 
 P = 128
 PACK = 4
+QUADS = 4
 ALIGN = 64
+BANKS = 8
+HALVES = N // P
+GPSIMD_QUADS = 3
+VECTOR_PICKS = 3
 
 
 def tile_list_twotab_agree_one_finalgate_kernel(
@@ -29,146 +34,143 @@ def tile_list_twotab_agree_one_finalgate_kernel(
     nc = tc.nc
     with ExitStack() as ctx:
         pool = ctx.enter_context(tc.tile_pool(name="keep", bufs=1))
-        psum = ctx.enter_context(tc.psum_pool(name="psum", bufs=8))
+        psum = ctx.enter_context(tc.psum_pool(name="psum", bufs=BANKS))
 
-        def sb(name, shape, dtype, tag=""):
-            return pool.tile(shape, dtype, name=name, align_bytes=ALIGN, tag=tag)
+        def sb(name, shape, dtype, reuse=""):
+            return pool.tile(shape, dtype, name=name, align_bytes=ALIGN, tag=reuse)
 
         def load_list(name, src):
             tile = pool.tile(list(src.shape), U16, name=name)
             nc.sync.dma_start(tile[:], src)
             return tile
 
-        def load_words(eng, name, src, width, tag=""):
-            tile = sb(name, [P, width], U32, tag=tag)
-            eng.dma_start(out=tile[:].bitcast(I32), in_=src[0].rearrange("p n t -> p (n t)").bitcast(I32))
+        def load_words(name, src, width, reuse=""):
+            tile = sb(name, [P, width], U32, reuse=reuse)
+            nc.sync.dma_start(out=tile[:].bitcast(I32), in_=src[0].rearrange("p n t -> p (n t)").bitcast(I32))
             return tile
 
-        def scale_tile(eng, name, width):
+        def scale_tile(engine, name, width):
             tile = sb(name, [P, width], U8)
-            eng.memset(tile[:].bitcast(I32), 0)
+            engine.memset(tile[:].bitcast(I32), 0)
             return tile
 
-        def load_scales(engs, tile, src):
-            for q in range(4):
-                engs[q].dma_start(
+        def load_scales(engine, tile, src, first=0, last=QUADS):
+            for q in range(first, last):
+                engine.dma_start(
                     out=tile[32 * q : 32 * q + 4, :].bitcast(I32),
                     in_=src[0, 4 * q : 4 * q + 4, :].bitcast(I32),
                 )
 
-        sy, sc, gp, ve = nc.sync, nc.scalar, nc.gpsimd, nc.vector
-        xo_s = scale_tile(ve, "xo_s", Z)
-        w2_s = scale_tile(gp, "w2_s", R)
-        xt_s = scale_tile(ve, "xt_s", T)
-        w_s = scale_tile(gp, "w_s", R)
-        wb_s = scale_tile(ve, "wb_s", N)
+        xo_s = scale_tile(nc.gpsimd, "xo_s", Z)
+        w_s = scale_tile(nc.gpsimd, "w_s", R)
+        w2_s = scale_tile(nc.vector, "w2_s", R)
+        xt_s = scale_tile(nc.vector, "xt_s", T)
+        wb_s = scale_tile(nc.vector, "wb_s", N)
+
         warm = sb("warm", [P, 2], F32)
-        nc.gpsimd.memset(warm[:, 0:1], 0.0)
+        nc.vector.memset(warm[:, 0:1], 0.0)
         nc.scalar.activation(out=warm[:, 1:2], in_=warm[:, 0:1], func=ACT.Sigmoid)
 
-        l2 = load_list("l2", offs2)
-        xo_w = load_words(sy, "xo_w", xo_words, Z)
-        w2_w = load_words(sc, "w2_w", w2_words, R)
-        load_scales([sy, sy, sy, sy], xo_s, xo_scales)
-        load_scales([sy, sy, sy, sy], w2_s, w2_scales)
-        l1 = load_list("l1", offs)
+        load_scales(nc.gpsimd, w_s, w_scales, last=GPSIMD_QUADS)
+        w2_w = load_words("w2_w", w2_words, R)
+        load_scales(nc.sync, xo_s, xo_scales)
+        list2 = load_list("list2", offs2)
+        load_scales(nc.sync, w2_s, w2_scales, last=1)
+        xo_w = load_words("xo_w", xo_words, Z)
+        load_scales(nc.sync, w2_s, w2_scales, first=1)
+        w_w = load_words("w_w", w_words, R)
+        list1 = load_list("list1", offs)
         xt_w = sb("xt_w", [P, T], U16)
-        sy.dma_start(out=xt_w[:].bitcast(I32), in_=xt_words[0].bitcast(I32))
-        w_w = load_words(sy, "w_w", w_words, R)
-        l4 = load_list("l4", offs4)
-        l3 = load_list("l3", offs3)
-        load_scales([sy, sy, sy, sy], xt_s, xt_scales)
-        load_scales([sy, sy, sy, sy], w_s, w_scales)
-        sg_t = sb("sg_t", [P, PACK], F32)
-        gp.dma_start(out=sg_t[:], in_=sg.rearrange("(p t) o -> p (t o)", t=PACK))
-        load_scales([sy,sy,sy,sy], wb_s, wb_scales)
+        nc.sync.dma_start(out=xt_w[:].bitcast(I32), in_=xt_words[0].bitcast(I32))
+        list4 = load_list("list4", offs4)
+        list3 = load_list("list3", offs3)
+        load_scales(nc.sync, w_s, w_scales, first=GPSIMD_QUADS)
+        load_scales(nc.sync, xt_s, xt_scales)
 
-        def deal(eng, name, src, dtype, tag=""):
-            tile = pool.tile([P, PACK, P], dtype, name=name, align_bytes=ALIGN, tag=tag)
-            dst = tile[:].rearrange("p t m -> p m t")
-            words = src[:].rearrange("p (m t) -> p m t", t=PACK)
-            if eng is sc:
-                eng.copy(out=dst, in_=words)
-            else:
-                eng.tensor_copy(out=dst, in_=words)
+        def deal(copy, name, src, dtype, reuse=""):
+            tile = sb(name, [P, PACK, P], dtype, reuse=reuse)
+            copy(out=tile[:].rearrange("p t m -> p m t"), in_=src[:].rearrange("p (m t) -> p m t", t=PACK))
             return tile
 
-        def gather(name, src, lst, dtype, n):
-            tile = sb(name, [P, n], dtype)
-            ve.tensor_copy(out=tile[:], in_=src[:].indirect(lst[:]))
+        def gather_packed(name, src, offsets, dtype):
+            tile = sb(name, [P, J], dtype)
+            nc.vector.tensor_copy(out=tile[:], in_=src[:].indirect(offsets[:]))
             return tile
 
-        w2_wd = deal(sc, "w2_wd", w2_w, U32)
-        xo_g = gather("xo_g", xo_w, l2, U32, J)
-        xo_sg = gather("xo_sg", xo_s, l2, U8, J)
-        w2_sd = deal(ve, "w2_sd", w2_s, U8)
-        w_wd = deal(sc, "w_wd", w_w, U32)
-        xt_g = gather("xt_g", xt_w, l1, U16, J)
-        xt_sg = gather("xt_sg", xt_s, l1, U8, J)
-        w_sd = deal(ve, "w_sd", w_s, U8)
+        w2_w_runs = deal(nc.scalar.copy, "w2_w_runs", w2_w, U32)
+        xo_s_picked = gather_packed("xo_s_picked", xo_s, list2, U8)
+        xo_w_picked = gather_packed("xo_w_picked", xo_w, list2, U32)
+        w2_s_runs = deal(nc.vector.tensor_copy, "w2_s_runs", w2_s, U8)
+        w_w_runs = deal(nc.scalar.copy, "w_w_runs", w_w, U32)
+        xt_w_picked = gather_packed("xt_w_picked", xt_w, list1, U16)
+        w_s_runs = deal(nc.vector.tensor_copy, "w_s_runs", w_s, U8, reuse="xt_w")
+        xt_s_picked = gather_packed("xt_s_picked", xt_s, list1, U8)
 
-        wb_w = load_words(sy, "wb_w", wb_words, N, tag="w2_s")
-        l5 = load_list("l5", offs5)
-        tz_t = [sb("tz%d" % h, [P, E], F32, tag=("w2_w", "w_w")[h]) for h in range(2)]
-        so_t = sb("so_t", [P, 2], F32)
-        bo_t = sb("bo_t", [P, 2], F32)
-        for h in range(2):
-            sy.dma_start(out=tz_t[h][:], in_=tz[h * P : (h + 1) * P, :])
-        with nc.allow_non_contiguous_dma(reason="one value a partition"):
-            gp.dma_start(out=so_t[:], in_=so.rearrange("(h p) o -> p (h o)", h=2))
-            gp.dma_start(out=bo_t[:], in_=bo.rearrange("(h p) o -> p (h o)", h=2))
+        sg_t = sb("sg_t", [P, PACK], F32, reuse="xo_s")
+        nc.sync.dma_start(out=sg_t[:], in_=sg.rearrange("(p t) o -> p (t o)", t=PACK))
+        load_scales(nc.sync, wb_s, wb_scales)
+        wb_w = load_words("wb_w", wb_words, N, reuse="w2_s")
+        list5 = load_list("list5", offs5)
 
-        b_sb = [sb("b%d" % t, [P, J], F32) for t in range(PACK)]
-        a_sb = [sb("a%d" % t, [P, J], F32) for t in range(PACK)]
-        u = sb("u", [P, PACK, O], F32, tag="w_s")
-        v = sb("v", [P, PACK, O], F32)
+        b_runs = [sb("b_run%d" % t, [P, J], F32, reuse="w_w" if t == 0 else "") for t in range(PACK)]
+        a_runs = [sb("a_run%d" % t, [P, J], F32) for t in range(PACK)]
+        b3 = sb("b3", [P, PACK, O], F32, reuse="xt_s")
+        b4 = sb("b4", [P, PACK, O], F32)
         sig = sb("sig", [P, PACK, O], F32)
-        big = sb("big", [P, PACK, O], F32)
-        for t in range(PACK):
-            acc = psum.tile([P, J], F32, name="acc")
-            nc.tensor.matmul_mx(out=acc[:], lhsT=w2_wd[:, t, :].bitcast(E4M3), lhsT_scale=w2_sd[:, t, :],
-                                rhs=xo_g[:].bitcast(E5M2), rhs_scale=xo_sg[:], start=True, stop=True)
-            sc.copy(out=b_sb[t][:], in_=acc[:])
-        for t in range(PACK):
-            acc = psum.tile([P, J], F32, name="acc")
-            nc.tensor.matmul_mx(out=acc[:], lhsT=w_wd[:, t, :].bitcast(E5M2), lhsT_scale=w_sd[:, t, :],
-                                rhs=xt_g[:].bitcast(E2M1), rhs_scale=xt_sg[:], start=True, stop=True)
-            ve.tensor_copy(out=a_sb[t][:], in_=acc[:])
-        for t in range(PACK):
-            sc.activation(out=v[:, t, :], in_=b_sb[t][:].indirect(l4[:]), func=ACT.Copy)
-            if t == 3:
-                sc.activation(out=u[:, t, :], in_=b_sb[t][:].indirect(l3[:]), func=ACT.Copy)
-            else:
-                ve.tensor_copy(out=u[:, t, :], in_=b_sb[t][:].indirect(l3[:]))
-        for t in range(PACK):
-            sc.activation(out=sig[:, t, :], in_=a_sb[t][:].indirect(l4[:]), func=ACT.Sigmoid,
-                          scale=sg_t[:, t : t + 1])
-        for t in range(0, PACK, 2):
-            ve.tensor_tensor(out=big[:, t : t + 2, :], in0=u[:, t : t + 2, :], in1=v[:, t : t + 2, :], op=ALU.max)
 
-        gate = sb("gate", [P, 2, O], F32, tag="sg_t")
-        for h in range(2):
-            sc.activation(out=gate[:, h, :], in_=tz_t[h][:].indirect(l5[:]), func=ACT.Sigmoid,
-                          bias=bo_t[:, h : h + 1], scale=so_t[:, h : h + 1])
+        for t in range(PACK):
+            acc = psum.tile([P, J], F32, name="acc")
+            nc.tensor.matmul_mx(out=acc[:], lhsT=w2_w_runs[:, t, :].bitcast(E4M3), lhsT_scale=w2_s_runs[:, t, :],
+                                rhs=xo_w_picked[:].bitcast(E5M2), rhs_scale=xo_s_picked[:], start=True, stop=True)
+            nc.scalar.copy(out=b_runs[t][:], in_=acc[:])
+        for t in range(PACK):
+            nc.scalar.activation(out=b4[:, t, :], in_=b_runs[t][:].indirect(list4[:]), func=ACT.Copy)
+            if t < VECTOR_PICKS:
+                nc.vector.tensor_copy(out=b3[:, t, :], in_=b_runs[t][:].indirect(list3[:]))
+            else:
+                nc.scalar.activation(out=b3[:, t, :], in_=b_runs[t][:].indirect(list3[:]), func=ACT.Copy)
+
+        tz_t = [sb("tz%d" % h, [P, E], F32, reuse=("w2_w", "w_w")[h]) for h in range(HALVES)]
+        so_t = sb("so_t", [P, HALVES], F32, reuse="xo_w")
+        bo_t = sb("bo_t", [P, HALVES], F32, reuse="w2_w_runs")
+        for h in range(HALVES):
+            nc.sync.dma_start(out=tz_t[h][:], in_=tz[h * P : (h + 1) * P, :])
+        with nc.allow_non_contiguous_dma(reason="one value a partition and half"):
+            nc.sync.dma_start(out=so_t[:], in_=so.rearrange("(h p) o -> p (h o)", h=HALVES))
+            nc.sync.dma_start(out=bo_t[:], in_=bo.rearrange("(h p) o -> p (h o)", h=HALVES))
+
+        for t in range(PACK):
+            acc = psum.tile([P, J], F32, name="acc")
+            nc.tensor.matmul_mx(out=acc[:], lhsT=w_w_runs[:, t, :].bitcast(E5M2), lhsT_scale=w_s_runs[:, t, :],
+                                rhs=xt_w_picked[:].bitcast(E2M1), rhs_scale=xt_s_picked[:], start=True, stop=True)
+            nc.vector.tensor_copy(out=a_runs[t][:], in_=acc[:])
+        for t in range(PACK):
+            nc.scalar.activation(out=sig[:, t, :], in_=a_runs[t][:].indirect(list4[:]), func=ACT.Sigmoid,
+                                 scale=sg_t[:, t : t + 1])
+
+        larger = sb("larger", [P, PACK, O], F32, reuse="w_w_runs")
+        nc.vector.tensor_tensor(out=larger[:], in0=b3[:], in1=b4[:], op=ALU.max)
+        gate = sb("gate", [P, HALVES, O], F32, reuse="xo_s")
+        for h in range(HALVES):
+            nc.scalar.activation(out=gate[:, h, :], in_=tz_t[h][:].indirect(list5[:]), func=ACT.Sigmoid,
+                                 bias=bo_t[:, h : h + 1], scale=so_t[:, h : h + 1])
+
         hid = sb("hid", [P, O, PACK], BF16)
         hid_w = sb("hid_w", [P, O], U32)
         hid_s = sb("hid_s", [P, O], U8)
-        H = O // 2
-        for c in range(2):
-            cols = slice(c * H, (c + 1) * H)
-            nc.vector.tensor_tensor(out=hid[:, cols, :], in0=big[:, :, cols].rearrange("p t o -> p o t"),
+        ranges = [slice(0, O // 2), slice(O // 2, O)]
+        for cols in ranges:
+            nc.vector.tensor_tensor(out=hid[:, cols, :], in0=larger[:, :, cols].rearrange("p t o -> p o t"),
                                     in1=sig[:, :, cols].rearrange("p t o -> p o t"), op=ALU.mult)
-        for c in range(2):
-            cols = slice(c * H, (c + 1) * H)
+        for cols in ranges:
             nc.vector.quantize_mx(out=hid_w[:, cols].bitcast(E5M2), scales=hid_s[:, cols],
                                   in_=hid[:, cols, :].rearrange("p o t -> p (o t)"))
 
-        res = sb("res", [P, 2, O], F32)
-        acc = psum.tile([P, J], F32, name="acc")
-        for h in range(2):
-            nc.tensor.matmul_mx(out=acc[:, h * O : (h + 1) * O], lhsT=wb_w[:, h * P : (h + 1) * P].bitcast(E4M3),
-                                lhsT_scale=wb_s[:, h * P : (h + 1) * P],
+        for h in range(HALVES):
+            rows = slice(h * P, (h + 1) * P)
+            acc = psum.tile([P, J], F32, name="acc")
+            nc.tensor.matmul_mx(out=acc[:, 0:O], lhsT=wb_w[:, rows].bitcast(E4M3), lhsT_scale=wb_s[:, rows],
                                 rhs=hid_w[:].bitcast(E5M2), rhs_scale=hid_s[:], start=True, stop=True)
-        nc.vector.tensor_tensor(out=res[:].rearrange("p h o -> p (h o)"), in0=acc[:],
-                                in1=gate[:].rearrange("p h o -> p (h o)"), op=ALU.mult)
-        nc.sync.dma_start(out=out.rearrange("(h p) o -> p h o", h=2), in_=res[:])
+            res = sb("res%d" % h, [P, O], F32)
+            nc.vector.tensor_tensor(out=res[:], in0=acc[:, 0:O], in1=gate[:, h, :], op=ALU.mult)
+            (nc.sync, nc.scalar)[h].dma_start(out=out[rows, :], in_=res[:])

from contextlib import ExitStack

import concourse.mybir as mybir

K, F, T, Z, J, R, O, N, E = 512, 512, 1024, 1024, 256, 512, 128, 256, 512
FLOPS = 2 * (K * R * J + F * R * J + R * N * O)

F32 = mybir.dt.float32
BF16 = mybir.dt.bfloat16
I32 = mybir.dt.int32
U32 = mybir.dt.uint32
U16 = mybir.dt.uint16
U8 = mybir.dt.uint8
E4M3 = mybir.dt.float8_e4m3fn_x4
E5M2 = mybir.dt.float8_e5m2_x4
E2M1 = mybir.dt.float4_e2m1fn_x4
ACT = mybir.ActivationFunctionType
ALU = mybir.AluOpType

P = 128
PACK = 4
QUADS = 4
ALIGN = 64
BANKS = 8
HALVES = N // P
GPSIMD_QUADS = 3
VECTOR_PICKS = 3


def tile_list_twotab_agree_one_finalgate_kernel(
    tc, xt_words, xt_scales, w_words, w_scales, xo_words, xo_scales, w2_words, w2_scales,
    sg, wb_words, wb_scales, tz, so, bo, offs, offs2, offs3, offs4, offs5, out,
):
    nc = tc.nc
    with ExitStack() as ctx:
        pool = ctx.enter_context(tc.tile_pool(name="keep", bufs=1))
        psum = ctx.enter_context(tc.psum_pool(name="psum", bufs=BANKS))

        def sb(name, shape, dtype, reuse=""):
            return pool.tile(shape, dtype, name=name, align_bytes=ALIGN, tag=reuse)

        def load_list(name, src):
            tile = pool.tile(list(src.shape), U16, name=name)
            nc.sync.dma_start(tile[:], src)
            return tile

        def load_words(name, src, width, reuse=""):
            tile = sb(name, [P, width], U32, reuse=reuse)
            nc.sync.dma_start(out=tile[:].bitcast(I32), in_=src[0].rearrange("p n t -> p (n t)").bitcast(I32))
            return tile

        def scale_tile(engine, name, width):
            tile = sb(name, [P, width], U8)
            engine.memset(tile[:].bitcast(I32), 0)
            return tile

        def load_scales(engine, tile, src, first=0, last=QUADS):
            for q in range(first, last):
                engine.dma_start(
                    out=tile[32 * q : 32 * q + 4, :].bitcast(I32),
                    in_=src[0, 4 * q : 4 * q + 4, :].bitcast(I32),
                )

        xo_s = scale_tile(nc.gpsimd, "xo_s", Z)
        w_s = scale_tile(nc.gpsimd, "w_s", R)
        w2_s = scale_tile(nc.vector, "w2_s", R)
        xt_s = scale_tile(nc.vector, "xt_s", T)
        wb_s = scale_tile(nc.vector, "wb_s", N)

        warm = sb("warm", [P, 2], F32)
        nc.vector.memset(warm[:, 0:1], 0.0)
        nc.scalar.activation(out=warm[:, 1:2], in_=warm[:, 0:1], func=ACT.Sigmoid)

        load_scales(nc.gpsimd, w_s, w_scales, last=GPSIMD_QUADS)
        w2_w = load_words("w2_w", w2_words, R)
        load_scales(nc.sync, xo_s, xo_scales)
        list2 = load_list("list2", offs2)
        load_scales(nc.sync, w2_s, w2_scales, last=1)
        xo_w = load_words("xo_w", xo_words, Z)
        load_scales(nc.sync, w2_s, w2_scales, first=1)
        w_w = load_words("w_w", w_words, R)
        list1 = load_list("list1", offs)
        xt_w = sb("xt_w", [P, T], U16)
        nc.sync.dma_start(out=xt_w[:].bitcast(I32), in_=xt_words[0].bitcast(I32))
        list4 = load_list("list4", offs4)
        list3 = load_list("list3", offs3)
        load_scales(nc.sync, w_s, w_scales, first=GPSIMD_QUADS)
        load_scales(nc.sync, xt_s, xt_scales)

        def deal(copy, name, src, dtype, reuse=""):
            tile = sb(name, [P, PACK, P], dtype, reuse=reuse)
            copy(out=tile[:].rearrange("p t m -> p m t"), in_=src[:].rearrange("p (m t) -> p m t", t=PACK))
            return tile

        def gather_packed(name, src, offsets, dtype):
            tile = sb(name, [P, J], dtype)
            nc.vector.tensor_copy(out=tile[:], in_=src[:].indirect(offsets[:]))
            return tile

        w2_w_runs = deal(nc.scalar.copy, "w2_w_runs", w2_w, U32)
        xo_s_picked = gather_packed("xo_s_picked", xo_s, list2, U8)
        xo_w_picked = gather_packed("xo_w_picked", xo_w, list2, U32)
        w2_s_runs = deal(nc.vector.tensor_copy, "w2_s_runs", w2_s, U8)
        w_w_runs = deal(nc.scalar.copy, "w_w_runs", w_w, U32)
        xt_w_picked = gather_packed("xt_w_picked", xt_w, list1, U16)
        w_s_runs = deal(nc.vector.tensor_copy, "w_s_runs", w_s, U8, reuse="xt_w")
        xt_s_picked = gather_packed("xt_s_picked", xt_s, list1, U8)

        sg_t = sb("sg_t", [P, PACK], F32, reuse="xo_s")
        nc.sync.dma_start(out=sg_t[:], in_=sg.rearrange("(p t) o -> p (t o)", t=PACK))
        load_scales(nc.sync, wb_s, wb_scales)
        wb_w = load_words("wb_w", wb_words, N, reuse="w2_s")
        list5 = load_list("list5", offs5)

        b_runs = [sb("b_run%d" % t, [P, J], F32, reuse="w_w" if t == 0 else "") for t in range(PACK)]
        a_runs = [sb("a_run%d" % t, [P, J], F32) for t in range(PACK)]
        b3 = sb("b3", [P, PACK, O], F32, reuse="xt_s")
        b4 = sb("b4", [P, PACK, O], F32)
        sig = sb("sig", [P, PACK, O], F32)

        for t in range(PACK):
            acc = psum.tile([P, J], F32, name="acc")
            nc.tensor.matmul_mx(out=acc[:], lhsT=w2_w_runs[:, t, :].bitcast(E4M3), lhsT_scale=w2_s_runs[:, t, :],
                                rhs=xo_w_picked[:].bitcast(E5M2), rhs_scale=xo_s_picked[:], start=True, stop=True)
            nc.scalar.copy(out=b_runs[t][:], in_=acc[:])
        for t in range(PACK):
            nc.scalar.activation(out=b4[:, t, :], in_=b_runs[t][:].indirect(list4[:]), func=ACT.Copy)
            if t < VECTOR_PICKS:
                nc.vector.tensor_copy(out=b3[:, t, :], in_=b_runs[t][:].indirect(list3[:]))
            else:
                nc.scalar.activation(out=b3[:, t, :], in_=b_runs[t][:].indirect(list3[:]), func=ACT.Copy)

        tz_t = [sb("tz%d" % h, [P, E], F32, reuse=("w2_w", "w_w")[h]) for h in range(HALVES)]
        so_t = sb("so_t", [P, HALVES], F32, reuse="xo_w")
        bo_t = sb("bo_t", [P, HALVES], F32, reuse="w2_w_runs")
        for h in range(HALVES):
            nc.sync.dma_start(out=tz_t[h][:], in_=tz[h * P : (h + 1) * P, :])
        with nc.allow_non_contiguous_dma(reason="one value a partition and half"):
            nc.sync.dma_start(out=so_t[:], in_=so.rearrange("(h p) o -> p (h o)", h=HALVES))
            nc.sync.dma_start(out=bo_t[:], in_=bo.rearrange("(h p) o -> p (h o)", h=HALVES))

        for t in range(PACK):
            acc = psum.tile([P, J], F32, name="acc")
            nc.tensor.matmul_mx(out=acc[:], lhsT=w_w_runs[:, t, :].bitcast(E5M2), lhsT_scale=w_s_runs[:, t, :],
                                rhs=xt_w_picked[:].bitcast(E2M1), rhs_scale=xt_s_picked[:], start=True, stop=True)
            nc.vector.tensor_copy(out=a_runs[t][:], in_=acc[:])
        for t in range(PACK):
            nc.scalar.activation(out=sig[:, t, :], in_=a_runs[t][:].indirect(list4[:]), func=ACT.Sigmoid,
                                 scale=sg_t[:, t : t + 1])

        larger = sb("larger", [P, PACK, O], F32, reuse="w_w_runs")
        nc.vector.tensor_tensor(out=larger[:], in0=b3[:], in1=b4[:], op=ALU.max)
        gate = sb("gate", [P, HALVES, O], F32, reuse="xo_s")
        for h in range(HALVES):
            nc.scalar.activation(out=gate[:, h, :], in_=tz_t[h][:].indirect(list5[:]), func=ACT.Sigmoid,
                                 bias=bo_t[:, h : h + 1], scale=so_t[:, h : h + 1])

        hid = sb("hid", [P, O, PACK], BF16)
        hid_w = sb("hid_w", [P, O], U32)
        hid_s = sb("hid_s", [P, O], U8)
        ranges = [slice(0, O // 2), slice(O // 2, O)]
        for cols in ranges:
            nc.vector.tensor_tensor(out=hid[:, cols, :], in0=larger[:, :, cols].rearrange("p t o -> p o t"),
                                    in1=sig[:, :, cols].rearrange("p t o -> p o t"), op=ALU.mult)
        for cols in ranges:
            nc.vector.quantize_mx(out=hid_w[:, cols].bitcast(E5M2), scales=hid_s[:, cols],
                                  in_=hid[:, cols, :].rearrange("p o t -> p (o t)"))

        for h in range(HALVES):
            rows = slice(h * P, (h + 1) * P)
            acc = psum.tile([P, J], F32, name="acc")
            nc.tensor.matmul_mx(out=acc[:, 0:O], lhsT=wb_w[:, rows].bitcast(E4M3), lhsT_scale=wb_s[:, rows],
                                rhs=hid_w[:].bitcast(E5M2), rhs_scale=hid_s[:], start=True, stop=True)
            res = sb("res%d" % h, [P, O], F32)
            nc.vector.tensor_tensor(out=res[:], in0=acc[:, 0:O], in1=gate[:, h, :], op=ALU.mult)
            (nc.sync, nc.scalar)[h].dma_start(out=out[rows, :], in_=res[:])
